import numpy as np, ml_dtypes
CORES = [7,15,23,31,167,175,183,191,327,335,343,351,487,495,503,511]
N = 16
G1 = [0,1,2,3,4,5,6,7]
G2 = [8,9,10,11,12,13,14,15]
def setup_inputs(rng):
    return {"x1": rng.standard_normal((N, 128, 128), dtype=np.float32).astype(ml_dtypes.bfloat16), "x2": rng.standard_normal((N, 128, 16), dtype=np.float32)}
def reference(x1, x2):
    out = {}
    y = np.full((N, 128, 128), np.nan, x1.dtype)
    for i, r in enumerate(G1):
        y[r] = np.concatenate([x1[s][:, 16 * i:16 * i + 16] for s in G1], axis=1)
    out["y1"] = y
    y = np.full((N, 128, 2), np.nan, x2.dtype)
    s = x2[G2].sum(axis=0, dtype=np.float64).astype(x2.dtype)
    for i, r in enumerate(G2):
        y[r] = s[:, 2 * i:2 * i + 2]
    out["y2"] = y
    return out

@@ -1,0 +1,76 @@
+from concourse.bass import DstId, RemoteDMATransfer
+
+SCRATCH = {
+    "xs": ("sbuf", [128, 128], "bfloat16"),
+    "land1": ("sbuf", [128, 128], "bfloat16"),
+    "d2": ("dram", [128, 16], "float32"),
+    "land2": ("dram", [8, 128, 16], "float32"),
+    "res2": ("dram", [128, 16], "float32"),
+}
+SEMAPHORES = ["ld", "own", "arr", "sent", "st"]
+
+
+def _dst(topo, d, core):
+    rid, pid = topo.addr(d, core)
+    return DstId(rid=rid, pnc=pid)
+
+
+def _all_to_all(g, core, T, topo, members, i):
+    B = 16
+    s = T.sem
+    g.sync.dma_start(T.xs[:], T.x1[:]).then_inc(s.ld, 16)
+    g.sync.dma_start(T.land1[:, B * i:B * i + B], T.x1[:, B * i:B * i + B]).then_inc(s.own, 16)
+    g.wait_ge(s.ld, 16)
+    trs = []
+    e = 0
+    for k in range(1, 8):
+        j = (i + k) % 8
+        trs.append(RemoteDMATransfer(dst_ids=[_dst(topo, members[j], core)], dma_engine_mask=1 << e, remote_sem=s.arr,
+                                     src=T.xs[:, B * j:B * j + B], dst=T.land1[:, B * i:B * i + B]))
+        e += 1
+    g.remote_dma_fused(trs, local_sem=s.sent)
+    g.sync.wait_ge(s.own, 16)
+    g.sync.wait_ge(s.arr, 7)
+    g.sync.dma_start(T.y1[:], T.land1[:]).then_inc(s.st, 16)
+    g.wait_ge(s.sent, 7)
+    g.wait_ge(s.st, 16)
+
+
+def _rs_member(g, core, T, topo, members, i):
+    s = T.sem
+    g.sync.dma_start(T.d2[:], T.x2[:]).then_inc(s.ld, 16)
+    g.wait_ge(s.ld, 16)
+    trs = []
+    e = 0
+    for k in range(1, 8):
+        j = (i + k) % 8
+        trs.append(RemoteDMATransfer(dst_ids=[_dst(topo, members[j] - 1, core)], dma_engine_mask=1 << e,
+                                     remote_sem=s.arr, src=T.d2[:], dst=T.land2[i]))
+        e += 1
+    trs.append(RemoteDMATransfer(dst_ids=[_dst(topo, core - 1, core)], dma_engine_mask=0xFF00, remote_sem=s.arr,
+                                 src=T.d2[:], dst=T.land2[i]))
+    g.remote_dma_fused(trs, local_sem=s.sent)
+    g.sync.wait_ge(s.arr, 16)
+    g.sync.dma_start(T.y2[:], T.res2[:, 2 * i:2 * i + 2]).then_inc(s.st, 16)
+    g.wait_ge(s.sent, 15)
+    g.wait_ge(s.st, 16)
+
+
+def _rs_helper(g, core, T, topo):
+    s = T.sem
+    g.wait_ge(s.arr, 15)
+    g.remote_dma_fused([RemoteDMATransfer(dst_ids=[_dst(topo, core + 1, core)], dma_engine_mask=0xFFFF,
+                                          remote_sem=s.arr, srcs=[T.land2[k] for k in range(8)], dsts=[T.res2[:]],
+                                          alu_op=1)], local_sem=s.sent)
+    g.wait_ge(s.sent, 16)
+
+
+def rank_program(g, core, T, topo):
+    m1 = [T.cores[r] for r in T.tables["G1"]]
+    m2 = [T.cores[r] for r in T.tables["G2"]]
+    if core in m1:
+        _all_to_all(g, core, T, topo, m1, m1.index(core))
+    elif core in m2:
+        _rs_member(g, core, T, topo, m2, m2.index(core))
+    elif core + 1 in m2:
+        _rs_helper(g, core, T, topo)

@@ -1,11 +1,15 @@
 from concourse.bass import DstId, RemoteDMATransfer
 
+K = 4
+W = 16 // K
+M = 8 // K
+
 SCRATCH = {
     "xs": ("sbuf", [128, 128], "bfloat16"),
     "land1": ("sbuf", [128, 128], "bfloat16"),
-    "d2": ("dram", [128, 16], "float32"),
-    "land2": ("dram", [8, 128, 16], "float32"),
-    "res2": ("dram", [128, 16], "float32"),
+    "d2": ("dram", [K, 128, W], "float32"),
+    "land2": ("dram", [8, 128, W], "float32"),
+    "res2": ("dram", [128, W], "float32"),
 }
 SEMAPHORES = ["ld", "own", "arr", "sent", "st"]
 
@@ -38,20 +42,23 @@ def _all_to_all(g, core, T, topo, members, i):
 
 def _rs_member(g, core, T, topo, members, i):
     s = T.sem
-    g.sync.dma_start(T.d2[:], T.x2[:]).then_inc(s.ld, 16)
-    g.wait_ge(s.ld, 16)
+    for q in range(K):
+        eng = g.sync if q % 2 == 0 else g.scalar
+        eng.dma_start(T.d2[q], T.x2[:, W * q:W * q + W]).then_inc(s.ld, 16)
+    g.wait_ge(s.ld, 16 * K)
     trs = []
     e = 0
     for k in range(1, 8):
         j = (i + k) % 8
         trs.append(RemoteDMATransfer(dst_ids=[_dst(topo, members[j] - 1, core)], dma_engine_mask=1 << e,
-                                     remote_sem=s.arr, src=T.d2[:], dst=T.land2[i]))
+                                     remote_sem=s.arr, src=T.d2[j // M], dst=T.land2[i]))
         e += 1
     trs.append(RemoteDMATransfer(dst_ids=[_dst(topo, core - 1, core)], dma_engine_mask=0xFF00, remote_sem=s.arr,
-                                 src=T.d2[:], dst=T.land2[i]))
+                                 src=T.d2[i // M], dst=T.land2[i]))
     g.remote_dma_fused(trs, local_sem=s.sent)
     g.sync.wait_ge(s.arr, 16)
-    g.sync.dma_start(T.y2[:], T.res2[:, 2 * i:2 * i + 2]).then_inc(s.st, 16)
+    c = 2 * (i % M)
+    g.sync.dma_start(T.y2[:], T.res2[:, c:c + 2]).then_inc(s.st, 16)
     g.wait_ge(s.sent, 15)
     g.wait_ge(s.st, 16)
 

@@ -3,15 +3,16 @@ from concourse.bass import DstId, RemoteDMATransfer
 K = 4
 W = 16 // K
 M = 8 // K
+B = 16
 
 SCRATCH = {
-    "xs": ("sbuf", [128, 128], "bfloat16"),
-    "land1": ("sbuf", [128, 128], "bfloat16"),
+    "d1": ("dram", [K, 128, M * B], "bfloat16"),
+    "land1": ("dram", [8, 128, M * B], "bfloat16"),
     "d2": ("dram", [K, 128, W], "float32"),
     "land2": ("dram", [8, 128, W], "float32"),
     "res2": ("dram", [128, W], "float32"),
 }
-SEMAPHORES = ["ld", "own", "arr", "sent", "st"]
+SEMAPHORES = ["ld", "arr", "sent", "st"]
 
 
 def _dst(topo, d, core):
@@ -20,52 +21,54 @@ def _dst(topo, d, core):
 
 
 def _all_to_all(g, core, T, topo, members, i):
-    B = 16
     s = T.sem
-    g.sync.dma_start(T.xs[:], T.x1[:]).then_inc(s.ld, 16)
-    g.sync.dma_start(T.land1[:, B * i:B * i + B], T.x1[:, B * i:B * i + B]).then_inc(s.own, 16)
-    g.wait_ge(s.ld, 16)
+    GW = M * B
+    qs = [g.sync, g.scalar]
+    for q in range(K):
+        qs[q % 2].dma_start(T.d1[q], T.x1[:, GW * q:GW * q + GW]).then_inc(s.ld, 16)
+    g.scalar.dma_start(T.y1[:, B * i:B * i + B], T.x1[:, B * i:B * i + B]).then_inc(s.st, 16)
+    g.wait_ge(s.ld, 16 * K)
     trs = []
-    e = 0
-    for k in range(1, 8):
-        j = (i + k) % 8
-        trs.append(RemoteDMATransfer(dst_ids=[_dst(topo, members[j], core)], dma_engine_mask=1 << e, remote_sem=s.arr,
-                                     src=T.xs[:, B * j:B * j + B], dst=T.land1[:, B * i:B * i + B]))
-        e += 1
+    for q in range(K):
+        ds = [j for j in range(M * q, M * q + M) if j != i]
+        trs.append(RemoteDMATransfer(dst_ids=[_dst(topo, members[j], core) for j in ds], dma_engine_mask=3 << (2 * q),
+                                     remote_sem=s.arr, srcs=[T.d1[q]], dsts=[T.land1[i] for j in ds]))
     g.remote_dma_fused(trs, local_sem=s.sent)
-    g.sync.wait_ge(s.own, 16)
-    g.sync.wait_ge(s.arr, 7)
-    g.sync.dma_start(T.y1[:], T.land1[:]).then_inc(s.st, 16)
-    g.wait_ge(s.sent, 7)
-    g.wait_ge(s.st, 16)
+    g.sync.wait_ge(s.arr, 14)
+    g.scalar.wait_ge(s.arr, 14)
+    h = B * (i % M)
+    n = 0
+    for j in range(8):
+        if j != i:
+            qs[n % 2].dma_start(T.y1[:, B * j:B * j + B], T.land1[j][:, h:h + B]).then_inc(s.st, 16)
+            n += 1
+    g.wait_ge(s.sent, 8)
+    g.wait_ge(s.st, 16 * 8)
 
 
 def _rs_member(g, core, T, topo, members, i):
     s = T.sem
+    qs = [g.sync, g.scalar]
     for q in range(K):
-        eng = g.sync if q % 2 == 0 else g.scalar
-        eng.dma_start(T.d2[q], T.x2[:, W * q:W * q + W]).then_inc(s.ld, 16)
+        qs[q % 2].dma_start(T.d2[q], T.x2[:, W * q:W * q + W]).then_inc(s.ld, 16)
     g.wait_ge(s.ld, 16 * K)
     trs = []
-    e = 0
-    for k in range(1, 8):
-        j = (i + k) % 8
-        trs.append(RemoteDMATransfer(dst_ids=[_dst(topo, members[j] - 1, core)], dma_engine_mask=1 << e,
-                                     remote_sem=s.arr, src=T.d2[j // M], dst=T.land2[i]))
-        e += 1
-    trs.append(RemoteDMATransfer(dst_ids=[_dst(topo, core - 1, core)], dma_engine_mask=0xFF00, remote_sem=s.arr,
-                                 src=T.d2[i // M], dst=T.land2[i]))
+    for q in range(K):
+        ds = list(range(M * q, M * q + M))
+        trs.append(RemoteDMATransfer(dst_ids=[_dst(topo, members[j] - 1, core) for j in ds],
+                                     dma_engine_mask=3 << (2 * q), remote_sem=s.arr, srcs=[T.d2[q]],
+                                     dsts=[T.land2[i] for j in ds]))
     g.remote_dma_fused(trs, local_sem=s.sent)
     g.sync.wait_ge(s.arr, 16)
     c = 2 * (i % M)
     g.sync.dma_start(T.y2[:], T.res2[:, c:c + 2]).then_inc(s.st, 16)
-    g.wait_ge(s.sent, 15)
+    g.wait_ge(s.sent, 8)
     g.wait_ge(s.st, 16)
 
 
 def _rs_helper(g, core, T, topo):
     s = T.sem
-    g.wait_ge(s.arr, 15)
+    g.wait_ge(s.arr, 16)
     g.remote_dma_fused([RemoteDMATransfer(dst_ids=[_dst(topo, core + 1, core)], dma_engine_mask=0xFFFF,
                                           remote_sem=s.arr, srcs=[T.land2[k] for k in range(8)], dsts=[T.res2[:]],
                                           alu_op=1)], local_sem=s.sent)

@@ -1,18 +1,22 @@
 from concourse.bass import DstId, RemoteDMATransfer
 
-K = 4
-W = 16 // K
-M = 8 // K
 B = 16
+K1 = 4
+M1 = 8 // K1
+E1 = 8 // K1
+K2 = 2
+M2 = 8 // K2
+W2 = 16 // K2
+E2 = 8 // K2
 
 SCRATCH = {
-    "d1": ("dram", [K, 128, M * B], "bfloat16"),
-    "land1": ("dram", [8, 128, M * B], "bfloat16"),
-    "d2": ("dram", [K, 128, W], "float32"),
-    "land2": ("dram", [8, 128, W], "float32"),
-    "res2": ("dram", [128, W], "float32"),
+    "d1": ("dram", [K1, 128, M1 * B], "bfloat16"),
+    "land1": ("dram", [8, 128, M1 * B], "bfloat16"),
+    "d2": ("dram", [K2, 128, W2], "float32"),
+    "land2": ("dram", [8, 128, W2], "float32"),
+    "res2": ("dram", [128, W2], "float32"),
 }
-SEMAPHORES = ["ld", "arr", "sent", "st"]
+SEMAPHORES = ["ld", "arr", "arr0", "arr1", "sent", "st"]
 
 
 def _dst(topo, d, core):
@@ -20,28 +24,38 @@ def _dst(topo, d, core):
     return DstId(rid=rid, pnc=pid)
 
 
+def _a2a_dests(topo, members, j, q):
+    pj = topo.chip(members[j]) % 2
+    ds = [d for d in range(M1 * q, M1 * q + M1) if d != j]
+    return sorted(ds, key=lambda d: topo.chip(members[d]) % 2 != pj)
+
+
 def _all_to_all(g, core, T, topo, members, i):
     s = T.sem
-    GW = M * B
+    GW = M1 * B
     qs = [g.sync, g.scalar]
-    for q in range(K):
+    arr = [s.arr0, s.arr1]
+    for q in range(K1):
         qs[q % 2].dma_start(T.d1[q], T.x1[:, GW * q:GW * q + GW]).then_inc(s.ld, 16)
     g.scalar.dma_start(T.y1[:, B * i:B * i + B], T.x1[:, B * i:B * i + B]).then_inc(s.st, 16)
-    g.wait_ge(s.ld, 16 * K)
+    g.wait_ge(s.ld, 16 * K1)
     trs = []
-    for q in range(K):
-        ds = [j for j in range(M * q, M * q + M) if j != i]
-        trs.append(RemoteDMATransfer(dst_ids=[_dst(topo, members[j], core) for j in ds], dma_engine_mask=3 << (2 * q),
-                                     remote_sem=s.arr, srcs=[T.d1[q]], dsts=[T.land1[i] for j in ds]))
+    for q in range(K1):
+        ds = _a2a_dests(topo, members, i, q)
+        trs.append(RemoteDMATransfer(dst_ids=[_dst(topo, members[d], core) for d in ds],
+                                     dma_engine_mask=((1 << E1) - 1) << (E1 * q),
+                                     remote_sem=arr[topo.chip(members[ds[0]]) % 2],
+                                     srcs=[T.d1[q]], dsts=[T.land1[i] for d in ds]))
     g.remote_dma_fused(trs, local_sem=s.sent)
-    g.sync.wait_ge(s.arr, 14)
-    g.scalar.wait_ge(s.arr, 14)
-    h = B * (i % M)
-    n = 0
-    for j in range(8):
-        if j != i:
+    par = topo.chip(core) % 2
+    early = [j for j in range(8) if j != i and _a2a_dests(topo, members, j, i // M1)[0] == i]
+    late = [j for j in range(8) if j != i and j not in early]
+    h = B * (i % M1)
+    for wave, sem in ((early, arr[par]), (late, arr[1 - par])):
+        for qu in qs:
+            qu.wait_ge(sem, E1 * len(wave))
+        for n, j in enumerate(wave):
             qs[n % 2].dma_start(T.y1[:, B * j:B * j + B], T.land1[j][:, h:h + B]).then_inc(s.st, 16)
-            n += 1
     g.wait_ge(s.sent, 8)
     g.wait_ge(s.st, 16 * 8)
 
@@ -49,18 +63,27 @@ def _all_to_all(g, core, T, topo, members, i):
 def _rs_member(g, core, T, topo, members, i):
     s = T.sem
     qs = [g.sync, g.scalar]
-    for q in range(K):
-        qs[q % 2].dma_start(T.d2[q], T.x2[:, W * q:W * q + W]).then_inc(s.ld, 16)
-    g.wait_ge(s.ld, 16 * K)
+    for q in range(K2):
+        qs[q % 2].dma_start(T.d2[q], T.x2[:, W2 * q:W2 * q + W2]).then_inc(s.ld, 16)
+    g.wait_ge(s.ld, 16 * K2)
+
+    def near(d):
+        c = members[d]
+        if c == core:
+            return 3
+        if topo.mates(c, core):
+            return 2
+        return 1 if topo.same_plane(c, core) else 0
+
     trs = []
-    for q in range(K):
-        ds = list(range(M * q, M * q + M))
-        trs.append(RemoteDMATransfer(dst_ids=[_dst(topo, members[j] - 1, core) for j in ds],
-                                     dma_engine_mask=3 << (2 * q), remote_sem=s.arr, srcs=[T.d2[q]],
-                                     dsts=[T.land2[i] for j in ds]))
+    for q in range(K2):
+        ds = sorted(range(M2 * q, M2 * q + M2), key=near)
+        trs.append(RemoteDMATransfer(dst_ids=[_dst(topo, members[d] - 1, core) for d in ds],
+                                     dma_engine_mask=((1 << E2) - 1) << (E2 * q), remote_sem=s.arr, srcs=[T.d2[q]],
+                                     dsts=[T.land2[i] for d in ds]))
     g.remote_dma_fused(trs, local_sem=s.sent)
     g.sync.wait_ge(s.arr, 16)
-    c = 2 * (i % M)
+    c = 2 * (i % M2)
     g.sync.dma_start(T.y2[:], T.res2[:, c:c + 2]).then_inc(s.st, 16)
     g.wait_ge(s.sent, 8)
     g.wait_ge(s.st, 16)
@@ -68,7 +91,7 @@ def _rs_member(g, core, T, topo, members, i):
 
 def _rs_helper(g, core, T, topo):
     s = T.sem
-    g.wait_ge(s.arr, 16)
+    g.wait_ge(s.arr, 8 * E2)
     g.remote_dma_fused([RemoteDMATransfer(dst_ids=[_dst(topo, core + 1, core)], dma_engine_mask=0xFFFF,
                                           remote_sem=s.arr, srcs=[T.land2[k] for k in range(8)], dsts=[T.res2[:]],
                                           alu_op=1)], local_sem=s.sent)

@@ -3,11 +3,11 @@ from concourse.bass import DstId, RemoteDMATransfer
 B = 16
 K1 = 4
 M1 = 8 // K1
-E1 = 8 // K1
 K2 = 2
 M2 = 8 // K2
 W2 = 16 // K2
-E2 = 8 // K2
+OFF = 0xFF
+NE = 8
 
 SCRATCH = {
     "d1": ("dram", [K1, 128, M1 * B], "bfloat16"),
@@ -16,7 +16,7 @@ SCRATCH = {
     "land2": ("dram", [8, 128, W2], "float32"),
     "res2": ("dram", [128, W2], "float32"),
 }
-SEMAPHORES = ["ld", "arr", "arr0", "arr1", "sent", "st"]
+SEMAPHORES = ["ld0", "ld1", "ld2", "ld3", "w0", "w1", "w2", "w3", "arr", "sent", "st"]
 
 
 def _dst(topo, d, core):
@@ -24,74 +24,63 @@ def _dst(topo, d, core):
     return DstId(rid=rid, pnc=pid)
 
 
-def _a2a_dests(topo, members, j, q):
-    pj = topo.chip(members[j]) % 2
-    ds = [d for d in range(M1 * q, M1 * q + M1) if d != j]
-    return sorted(ds, key=lambda d: topo.chip(members[d]) % 2 != pj)
+def _near(topo, c, core):
+    if (topo.host(c), topo.chip(c)) == (topo.host(core), topo.chip(core)):
+        return 3
+    if topo.mates(c, core):
+        return 2
+    return 1 if topo.same_plane(c, core) else 0
 
 
 def _all_to_all(g, core, T, topo, members, i):
     s = T.sem
     GW = M1 * B
+    a = i // M1
     qs = [g.sync, g.scalar]
-    arr = [s.arr0, s.arr1]
-    for q in range(K1):
-        qs[q % 2].dma_start(T.d1[q], T.x1[:, GW * q:GW * q + GW]).then_inc(s.ld, 16)
+    order = [(a + 1 + p) % K1 for p in range(K1)]
+    for p, q in enumerate(order):
+        qs[p % 2].dma_start(T.d1[q], T.x1[:, GW * q:GW * q + GW]).then_inc(s["ld%d" % p], 16)
     g.scalar.dma_start(T.y1[:, B * i:B * i + B], T.x1[:, B * i:B * i + B]).then_inc(s.st, 16)
-    g.wait_ge(s.ld, 16 * K1)
-    trs = []
-    for q in range(K1):
-        ds = _a2a_dests(topo, members, i, q)
-        trs.append(RemoteDMATransfer(dst_ids=[_dst(topo, members[d], core) for d in ds],
-                                     dma_engine_mask=((1 << E1) - 1) << (E1 * q),
-                                     remote_sem=arr[topo.chip(members[ds[0]]) % 2],
-                                     srcs=[T.d1[q]], dsts=[T.land1[i] for d in ds]))
-    g.remote_dma_fused(trs, local_sem=s.sent)
-    par = topo.chip(core) % 2
-    early = [j for j in range(8) if j != i and _a2a_dests(topo, members, j, i // M1)[0] == i]
-    late = [j for j in range(8) if j != i and j not in early]
+    for p, q in enumerate(order):
+        ds = sorted([d for d in range(M1 * q, M1 * q + M1) if d != i], key=lambda d: _near(topo, members[d], core))
+        g.wait_ge(s["ld%d" % p], 16)
+        g.remote_dma_fused([RemoteDMATransfer(dst_ids=[_dst(topo, members[d], core) for d in ds], dma_engine_mask=OFF,
+                                              remote_sem=s["w%d" % p], srcs=[T.d1[q]],
+                                              dsts=[T.land1[i] for d in ds])], local_sem=s.sent)
     h = B * (i % M1)
-    for wave, sem in ((early, arr[par]), (late, arr[1 - par])):
-        for qu in qs:
-            qu.wait_ge(sem, E1 * len(wave))
-        for n, j in enumerate(wave):
+    for p in range(K1):
+        b = (a - 1 - p) % K1
+        senders = [j for j in range(M1 * b, M1 * b + M1) if j != i]
+        for n, j in enumerate(senders):
+            qs[n % 2].wait_ge(s["w%d" % p], NE * len(senders))
             qs[n % 2].dma_start(T.y1[:, B * j:B * j + B], T.land1[j][:, h:h + B]).then_inc(s.st, 16)
-    g.wait_ge(s.sent, 8)
+    g.wait_ge(s.sent, NE * K1)
     g.wait_ge(s.st, 16 * 8)
 
 
 def _rs_member(g, core, T, topo, members, i):
     s = T.sem
+    a = i // M2
     qs = [g.sync, g.scalar]
-    for q in range(K2):
-        qs[q % 2].dma_start(T.d2[q], T.x2[:, W2 * q:W2 * q + W2]).then_inc(s.ld, 16)
-    g.wait_ge(s.ld, 16 * K2)
-
-    def near(d):
-        c = members[d]
-        if c == core:
-            return 3
-        if topo.mates(c, core):
-            return 2
-        return 1 if topo.same_plane(c, core) else 0
-
-    trs = []
-    for q in range(K2):
-        ds = sorted(range(M2 * q, M2 * q + M2), key=near)
-        trs.append(RemoteDMATransfer(dst_ids=[_dst(topo, members[d] - 1, core) for d in ds],
-                                     dma_engine_mask=((1 << E2) - 1) << (E2 * q), remote_sem=s.arr, srcs=[T.d2[q]],
-                                     dsts=[T.land2[i] for d in ds]))
-    g.remote_dma_fused(trs, local_sem=s.sent)
+    order = [(a + 1 + p) % K2 for p in range(K2)]
+    for p, q in enumerate(order):
+        qs[p % 2].dma_start(T.d2[q], T.x2[:, W2 * q:W2 * q + W2]).then_inc(s["ld%d" % p], 16)
+    for p, q in enumerate(order):
+        ds = sorted(range(M2 * q, M2 * q + M2), key=lambda d: _near(topo, members[d], core))
+        g.wait_ge(s["ld%d" % p], 16)
+        g.remote_dma_fused([RemoteDMATransfer(dst_ids=[_dst(topo, members[d] - 1, core) for d in ds],
+                                              dma_engine_mask=OFF, remote_sem=s.arr, srcs=[T.d2[q]],
+                                              dsts=[T.land2[i] for d in ds])], local_sem=s.sent)
     g.sync.wait_ge(s.arr, 16)
     c = 2 * (i % M2)
     g.sync.dma_start(T.y2[:], T.res2[:, c:c + 2]).then_inc(s.st, 16)
-    g.wait_ge(s.sent, 8)
+    g.wait_ge(s.sent, NE * K2)
     g.wait_ge(s.st, 16)
 
 
 def _rs_helper(g, core, T, topo):
     s = T.sem
-    g.wait_ge(s.arr, 8 * E2)
+    g.wait_ge(s.arr, 8 * NE)
     g.remote_dma_fused([RemoteDMATransfer(dst_ids=[_dst(topo, core + 1, core)], dma_engine_mask=0xFFFF,
                                           remote_sem=s.arr, srcs=[T.land2[k] for k in range(8)], dsts=[T.res2[:]],
                                           alu_op=1)], local_sem=s.sent)

from concourse.bass import DstId, RemoteDMATransfer

B = 16
K1 = 4
M1 = 8 // K1
K2 = 2
M2 = 8 // K2
W2 = 16 // K2
OFF = 0xFF
NE = 8

SCRATCH = {
    "d1": ("dram", [K1, 128, M1 * B], "bfloat16"),
    "land1": ("dram", [8, 128, M1 * B], "bfloat16"),
    "d2": ("dram", [K2, 128, W2], "float32"),
    "land2": ("dram", [8, 128, W2], "float32"),
    "res2": ("dram", [128, W2], "float32"),
}
SEMAPHORES = ["ld0", "ld1", "ld2", "ld3", "w0", "w1", "w2", "w3", "arr", "sent", "st"]


def _dst(topo, d, core):
    rid, pid = topo.addr(d, core)
    return DstId(rid=rid, pnc=pid)


def _near(topo, c, core):
    if (topo.host(c), topo.chip(c)) == (topo.host(core), topo.chip(core)):
        return 3
    if topo.mates(c, core):
        return 2
    return 1 if topo.same_plane(c, core) else 0


def _all_to_all(g, core, T, topo, members, i):
    s = T.sem
    GW = M1 * B
    a = i // M1
    qs = [g.sync, g.scalar]
    order = [(a + 1 + p) % K1 for p in range(K1)]
    for p, q in enumerate(order):
        qs[p % 2].dma_start(T.d1[q], T.x1[:, GW * q:GW * q + GW]).then_inc(s["ld%d" % p], 16)
    g.scalar.dma_start(T.y1[:, B * i:B * i + B], T.x1[:, B * i:B * i + B]).then_inc(s.st, 16)
    for p, q in enumerate(order):
        ds = sorted([d for d in range(M1 * q, M1 * q + M1) if d != i], key=lambda d: _near(topo, members[d], core))
        g.wait_ge(s["ld%d" % p], 16)
        g.remote_dma_fused([RemoteDMATransfer(dst_ids=[_dst(topo, members[d], core) for d in ds], dma_engine_mask=OFF,
                                              remote_sem=s["w%d" % p], srcs=[T.d1[q]],
                                              dsts=[T.land1[i] for d in ds])], local_sem=s.sent)
    h = B * (i % M1)
    for p in range(K1):
        b = (a - 1 - p) % K1
        senders = [j for j in range(M1 * b, M1 * b + M1) if j != i]
        for n, j in enumerate(senders):
            qs[n % 2].wait_ge(s["w%d" % p], NE * len(senders))
            qs[n % 2].dma_start(T.y1[:, B * j:B * j + B], T.land1[j][:, h:h + B]).then_inc(s.st, 16)
    g.wait_ge(s.sent, NE * K1)
    g.wait_ge(s.st, 16 * 8)


def _rs_member(g, core, T, topo, members, i):
    s = T.sem
    a = i // M2
    qs = [g.sync, g.scalar]
    order = [(a + 1 + p) % K2 for p in range(K2)]
    for p, q in enumerate(order):
        qs[p % 2].dma_start(T.d2[q], T.x2[:, W2 * q:W2 * q + W2]).then_inc(s["ld%d" % p], 16)
    for p, q in enumerate(order):
        ds = sorted(range(M2 * q, M2 * q + M2), key=lambda d: _near(topo, members[d], core))
        g.wait_ge(s["ld%d" % p], 16)
        g.remote_dma_fused([RemoteDMATransfer(dst_ids=[_dst(topo, members[d] - 1, core) for d in ds],
                                              dma_engine_mask=OFF, remote_sem=s.arr, srcs=[T.d2[q]],
                                              dsts=[T.land2[i] for d in ds])], local_sem=s.sent)
    g.sync.wait_ge(s.arr, 16)
    c = 2 * (i % M2)
    g.sync.dma_start(T.y2[:], T.res2[:, c:c + 2]).then_inc(s.st, 16)
    g.wait_ge(s.sent, NE * K2)
    g.wait_ge(s.st, 16)


def _rs_helper(g, core, T, topo):
    s = T.sem
    g.wait_ge(s.arr, 8 * NE)
    g.remote_dma_fused([RemoteDMATransfer(dst_ids=[_dst(topo, core + 1, core)], dma_engine_mask=0xFFFF,
                                          remote_sem=s.arr, srcs=[T.land2[k] for k in range(8)], dsts=[T.res2[:]],
                                          alu_op=1)], local_sem=s.sent)
    g.wait_ge(s.sent, 16)


def rank_program(g, core, T, topo):
    m1 = [T.cores[r] for r in T.tables["G1"]]
    m2 = [T.cores[r] for r in T.tables["G2"]]
    if core in m1:
        _all_to_all(g, core, T, topo, m1, m1.index(core))
    elif core in m2:
        _rs_member(g, core, T, topo, m2, m2.index(core))
    elif core + 1 in m2:
        _rs_helper(g, core, T, topo)
